import numpy as np, ml_dtypes
CORES = [1,5,17,21,33,37,49,53]
N = 8
import mx_ref
BF = ml_dtypes.bfloat16
def entries(a):
    return np.ascontiguousarray(a.T).reshape(-1)
def table(e):
    return np.ascontiguousarray(np.reshape(e, (-1, 16)).T).astype(np.int32)
def gpick(z, e):
    return np.concatenate([z[16 * g:16 * g + 16][:, e[g]] for g in range(8)])
def tile(rs):
    return np.stack(rs, axis=2).reshape(128, -1).astype(BF)
def cut(t, i, w=512):
    return t[:, w * i:w * i + w]
def f(rng, *shape):
    return mx_ref.flush((rng.standard_normal(shape, dtype=np.float32) * np.exp2(rng.integers(-2, 3, shape[:-1] + (1,)))).astype(BF))
def wide(rng, *shape, cols=0):
    v = rng.standard_normal(shape, dtype=np.float32) * np.exp2(rng.integers(-12, 13, shape)).astype(np.float32)
    if cols: v *= np.repeat(np.exp2(rng.integers(-cols, cols + 1, shape[:-2] + (1, shape[-1] // 4))) * (rng.random(shape[:-2] + (1, shape[-1] // 4)) > 0.0625), 4, axis=-1).astype(np.float32)
    return mx_ref.flush(v.astype(BF))
TQ, O = 128, 1
def lay(k, q):
    return {"kp": np.repeat(k, 16, axis=1).astype(np.int32), "qp": np.stack([table(e) for e in q])}
def setup_inputs(rng):
    d = {"qx": f(rng, N, 128, 4 * TQ), "ky": f(rng, N, 128, 2048), "rt": np.repeat(f(rng, 1, 128, 1024), N, axis=0), "vv": f(rng, N, 128, 512 * O)}
    a = rng.integers(0, 3585)
    k = a + rng.integers(0, 512, (N, 8, 4))
    q = np.where(rng.random((N, TQ)) < 0.25, rng.integers(0, 4096, (N, TQ)), a + rng.integers(0, 512, (N, TQ)))
    return {**d, **lay(k, q)}
def setup_inputs_far(rng):
    d = setup_inputs(rng)
    k = rng.integers(1500, 2501, (N, 32)); q = np.zeros((N, TQ), int); a = int(rng.integers(0, 2))
    for r in range(N):
        k[r, rng.permutation(32)[:2]] = [1500, 2500]
        lo, hi = (2628, 4095) if (r + a) % 2 else (0, 1371)
        q[r] = rng.integers(lo, hi + 1, TQ)
        q[r, rng.permutation(TQ)[:2]] = [lo, hi]
    return {**d, **lay(k.reshape(N, 8, 4), q)}
def setup_inputs_same(rng):
    d = setup_inputs(rng); a = int(rng.integers(0, 4096))
    return {**d, **lay(np.full((N, 8, 4), a), np.full((N, TQ), a))}
def setup_inputs_descending(rng):
    d = setup_inputs(rng); a = rng.integers(0, 3585)
    q = np.stack([a + np.sort(rng.permutation(512)[:TQ])[::-1] for r in range(N)])
    k = np.stack([a + 16 * rng.permutation(32) + rng.integers(0, 16, 32) for r in range(N)])
    return {**d, **lay(k.reshape(N, 8, 4), q)}
def setup_inputs_near(rng):
    d = setup_inputs(rng); a = rng.integers(2049, 3968)
    q = np.stack([a + rng.permutation(TQ) % 128 for r in range(N)])
    k = np.stack([a + rng.permutation(np.concatenate([[0, 128], 1 + rng.permutation(127)[:30]])) for r in range(N)])
    return {**d, **lay(k.reshape(N, 8, 4), q)}
def setup_inputs_spread(rng):
    d = setup_inputs(rng); d["qx"] = wide(rng, N, 128, 4 * TQ, cols=4); return d
def check_inputs(d):
    b = []
    for r in range(N):
        k, q = d["kp"][r], entries(d["qp"][r])
        if d["rt"][r].tobytes() != d["rt"][0].tobytes(): b.append("rt")
        if k.min() < 0 or k.max() > 4095 or (k != np.repeat(k[::16], 16, axis=0)).any(): b.append("kp")
        if q.min() < 0 or q.max() > 4095: b.append("qp")
    return b
def reference(qx, ky, rt, vv, kp, qp):
    y = np.zeros((N, 128, O * TQ), np.float32)
    X = [mx_ref.quantize(qx[r]) for r in range(N)]
    for s in range(N):
        K = [mx_ref.quantize(np.ascontiguousarray(cut(ky[s], b))) for b in range(4)]
        V = [mx_ref.quantize(np.ascontiguousarray(cut(vv[s], o))) for o in range(O)]
        R = mx_ref.quantize(rt[s])
        P = [mx_ref.matmul(K[b], R) for b in range(4)]
        for r in range(N):
            A = []
            for b in range(4):
                c = np.clip(entries(qp[r])[None, :] - kp[s][::16, b][:, None], -128, 127) + 128
                A.append(np.maximum(mx_ref.matmul(K[b], X[r]) + gpick(P[b], c), np.float32(0)) * np.float32(0.03125))
            A = mx_ref.quantize(tile(A))
            for o in range(O): y[r][:, TQ * o:TQ * o + TQ] += mx_ref.matmul(V[o], A)
    return {"y": y}

@@ -1,0 +1,244 @@
+from concourse.bass import DstId, RemoteDMATransfer
+from concourse.mybir import dt, AluOpType, ActivationFunctionType
+
+C4, U8 = "float8_e4m3fn_x4", "uint8"
+SCRATCH = {
+    "xb": ("sbuf", [128, 1536], "bfloat16"),
+    "kb": ("sbuf", [128, 2560], "bfloat16"),
+    "xc": ("sbuf", [128, 512], C4),
+    "xs": ("sbuf", [128, 512], U8),
+    "kc": ("sbuf", [128, 896], C4),
+    "ks": ("sbuf", [128, 896], U8),
+    "fc": ("sbuf", [128, 640], C4),
+    "fs": ("sbuf", [128, 640], U8),
+    "lc": ("sbuf", [128, 2048], C4),
+    "ls": ("sbuf", [128, 2048], U8),
+    "qpi": ("sbuf", [128, 8], "int32"),
+    "qp16": ("sbuf", [128, 16], "uint16"),
+    "kpi": ("sbuf", [128, 4], "int32"),
+    "kpf": ("sbuf", [128, 4], "float32"),
+    "dd": ("sbuf", [128, 64], "float32"),
+    "off": ("sbuf", [128, 64], "uint16"),
+    "pp": ("sbuf", [128, 1024], "float32"),
+    "pg": ("sbuf", [128, 1024], "float32"),
+    "hh": ("sbuf", [128, 1024], "bfloat16"),
+    "yo": ("sbuf", [128, 128], "float32"),
+    "ps": ("psum", [128, 4096], "float32"),
+}
+SEMAPHORES = (["lkp", "lqp", "lqx", "lrt", "lvv", "lk0", "lk1", "ckp", "cqp", "zqx", "zrt", "zvv", "zk0", "zk1",
+               "akp", "aqo", "aqt", "xoc", "xop", "xtc", "xtp", "kvc", "kvp", "fwc", "fwp", "sent",
+               "dl", "ofs", "clp", "qa", "yd", "yc", "yst"]
+              + ["%s%d" % (n, b) for n in ("mp", "ms", "cp", "ga", "ad") for b in range(4)]
+              + ["av%d" % s for s in range(8)])
+
+
+def rank_program(g, core, T, topo):
+    S = T.sem
+    chips = []
+    for c in T.cores:
+        if topo.chip(c) not in chips:
+            chips.append(topo.chip(c))
+    if topo.chip(core) not in chips:
+        return
+    n = len(chips)
+
+    def rank_at(i, d):
+        return [c for c in T.cores if topo.chip(c) == chips[i % n] and topo.die(c) == d][0]
+
+    def helpers(r):
+        return [c for c in topo.cores_of(r) if topo.die(c) == topo.die(r) and c != r]
+
+    me, d = chips.index(topo.chip(core)), topo.die(core)
+    own, oth = rank_at(me, d), rank_at(me, 1 - d)
+    F, G, H = helpers(own)
+    oF, oG, oH = helpers(oth)
+    far = rank_at(me + 1, d)
+    lo = topo.engines(core, far)
+    near = topo.engines(core, own if core != own else oth)
+    hi = [e for e in near if e not in lo]
+    LO, HI, ALL = [sum(1 << e for e in es) for es in (lo, hi, near)]
+    n_lo, n_hi, n_all = len(lo), len(hi), len(near)
+    is_rank = core == own
+    src = own if is_rank else rank_at(me - {H: 1, G: 2, F: 3}[core], d)
+    srank = T.rank_of(src)
+    sent = [0]
+
+    def tr(mask, sem, src_ap, dests):
+        ids = []
+        for c, _ in dests:
+            rid, pid, _e = topo.addr(c)
+            ids.append(DstId(rid=rid, pnc=pid))
+        sent[0] += bin(mask).count("1")
+        return RemoteDMATransfer(dst_ids=ids, dma_engine_mask=mask, remote_sem=sem, srcs=[src_ap], dsts=[ap for _, ap in dests])
+
+    def send(*ts):
+        g.remote_dma_fused(list(ts), local_sem=S.sent)
+
+    def code(t, i, j):
+        return t[:, i:j].bitcast(dt.uint8)
+
+    sub, add, mx, mn, mult = AluOpType.subtract, AluOpType.add, AluOpType.max, AluOpType.min, AluOpType.mult
+    copy = ActivationFunctionType.Copy
+    v, a, te = g.vector, g.scalar, g.tensor
+
+    if is_rank:
+        g.scalar.dma_start(T.kpi[:], T.kp[:]).then_inc(S.lkp, 16)
+        g.sync.dma_start(T.xb[:, 1024:1536], T.qx[:]).then_inc(S.lqx, 16)
+        g.scalar.dma_start(T.xb[:, 0:1024], T.rt[:]).then_inc(S.lrt, 16)
+        g.sync.dma_start(T.kb[:, 512:1536], T.ky[:, 0:1024]).then_inc(S.lk0, 16)
+        for k in range(8):
+            q = g.sync if k % 2 else g.scalar
+            q.dma_start(T.qpi[16 * k:16 * k + 16, :], T.qp[:]).then_inc(S.lqp, 16)
+        g.scalar.dma_start(T.kb[:, 1536:2560], T.ky[:, 1024:2048]).then_inc(S.lk1, 16)
+        g.sync.dma_start(T.kb[:, 0:512], T.vv[:]).then_inc(S.lvv, 16)
+
+        v.wait_ge(S.lkp, 16)
+        v.tensor_copy(T.kpf[:], T.kpi[:]).then_inc(S.ckp, 1)
+        v.wait_ge(S.lqx, 16)
+        v.quantize_mx(T.xc[:, 256:384], T.xs[:, 256:384], T.xb[:, 1024:1536]).then_inc(S.zqx, 1)
+        v.wait_ge(S.lrt, 16)
+        v.quantize_mx(T.xc[:, 0:256], T.xs[:, 0:256], T.xb[:, 0:1024]).then_inc(S.zrt, 1)
+        v.wait_ge(S.lqp, 128)
+        v.tensor_copy(T.qp16[:, 0:8], T.qpi[:]).then_inc(S.cqp, 1)
+        v.wait_ge(S.lk0, 16)
+        v.quantize_mx(T.kc[:, 384:640], T.ks[:, 384:640], T.kb[:, 512:1536]).then_inc(S.zk0, 1)
+        v.wait_ge(S.lk1, 16)
+        v.quantize_mx(T.kc[:, 640:896], T.ks[:, 640:896], T.kb[:, 1536:2560]).then_inc(S.zk1, 1)
+        v.wait_ge(S.lvv, 16)
+        v.quantize_mx(T.kc[:, 256:384], T.ks[:, 256:384], T.kb[:, 0:512]).then_inc(S.zvv, 1)
+
+        one, two, three = helpers(rank_at(me + 1, d))[2], helpers(rank_at(me + 2, d))[1], helpers(rank_at(me + 3, d))[0]
+        g.wait_ge(S.ckp, 1)
+        send(tr(LO, S.akp, T.kpf[:], [(one, T.kpf[:]), (two, T.kpf[:]), (three, T.kpf[:])]))
+        g.wait_ge(S.zqx, 1)
+        g.wait_ge(S.zrt, 1)
+        send(tr(ALL, S.xoc, code(T.xc, 0, 384), [(F, code(T.xc, 0, 384))]))
+        send(tr(ALL, S.xop, T.xs[:, 0:384], [(F, T.xs[:, 0:384])]))
+        g.wait_ge(S.cqp, 1)
+        send(tr(HI, S.aqo, T.qp16[:, 0:8], [(F, T.qp16[:, 0:8])]))
+        g.wait_ge(S.zk0, 1)
+        g.wait_ge(S.zk1, 1)
+        g.wait_ge(S.zvv, 1)
+        send(tr(LO, S.kvc, code(T.kc, 256, 896), [(one, code(T.kc, 256, 896)), (two, code(T.kc, 256, 896))]),
+             tr(HI, S.fwc, code(T.kc, 256, 896), [(G, code(T.fc, 0, 640))]))
+        send(tr(LO, S.kvp, T.ks[:, 256:896], [(one, T.ks[:, 256:896]), (two, T.ks[:, 256:896])]),
+             tr(HI, S.fwp, T.ks[:, 256:896], [(G, T.fs[:, 0:640])]))
+    elif core == F:
+        g.wait_ge(S.xoc, n_all)
+        send(tr(LO, S.xtc, code(T.xc, 256, 384), [(c, code(T.xc, 384, 512)) for c in (oth, oF)]),
+             tr(HI, S.xtc, code(T.xc, 256, 384), [(c, code(T.xc, 384, 512)) for c in (oG, oH)]))
+        g.wait_ge(S.xop, n_all)
+        send(tr(LO, S.xtp, T.xs[:, 256:384], [(c, T.xs[:, 384:512]) for c in (oth, oF)]),
+             tr(HI, S.xtp, T.xs[:, 256:384], [(c, T.xs[:, 384:512]) for c in (oG, oH)]))
+        g.wait_ge(S.aqo, n_hi)
+        send(tr(LO, S.aqo, T.qp16[:, 0:8], [(c, T.qp16[:, 0:8]) for c in (G, H)]),
+             tr(HI, S.aqt, T.qp16[:, 0:8], [(c, T.qp16[:, 8:16]) for c in (oth, oF, oG, oH)]))
+        send(tr(LO, S.xoc, code(T.xc, 0, 384), [(H, code(T.xc, 0, 384))]),
+             tr(HI, S.xoc, code(T.xc, 0, 384), [(G, code(T.xc, 0, 384))]))
+        send(tr(LO, S.xop, T.xs[:, 0:384], [(H, T.xs[:, 0:384])]),
+             tr(HI, S.xop, T.xs[:, 0:384], [(G, T.xs[:, 0:384])]))
+    elif core == G:
+        three = helpers(rank_at(me + 3, d))[0]
+        g.wait_ge(S.fwc, n_hi)
+        send(tr(LO, S.kvc, code(T.fc, 0, 640), [(three, code(T.kc, 256, 896))]))
+        g.wait_ge(S.fwp, n_hi)
+        send(tr(LO, S.kvp, T.fs[:, 0:640], [(three, T.ks[:, 256:896])]))
+
+    if is_rank:
+        v.wait_ge(S.ckp, 1)
+        v.wait_ge(S.cqp, 1)
+    else:
+        v.wait_ge(S.akp, n_lo)
+        v.wait_ge(S.aqo, n_hi if core == F else n_lo)
+    v.wait_ge(S.aqt, n_hi)
+    for b in range(4):
+        v.tensor_scalar(T.dd[:, 16 * b:16 * b + 16], T.qp16[:], T.kpf[:, b:b + 1], -128.0, sub, mx).then_inc(S.dl, 1)
+    v.wait_ge(S.dl, 4)
+    v.tensor_scalar(T.off[:], T.dd[:], 127.0, 128.0, mn, add).then_inc(S.ofs, 1)
+
+    def stat(b):
+        return T.kc[:, 384 + 128 * b:512 + 128 * b], T.ks[:, 384 + 128 * b:512 + 128 * b]
+
+    def cut(t, b):
+        return t[:, 256 * b:256 * b + 256]
+
+    def bank(b):
+        return T.ps[:, 512 * b:512 * b + 256]
+
+    if is_rank:
+        te.wait_ge(S.zrt, 1)
+        te.wait_ge(S.zqx, 1)
+        te.wait_ge(S.zk0, 1)
+        te.wait_ge(S.zk1, 1)
+    else:
+        n_x = n_all if core == F else n_lo if core == H else n_hi
+        n_k = n_lo
+        te.wait_ge(S.xoc, n_x)
+        te.wait_ge(S.xop, n_x)
+        te.wait_ge(S.kvc, n_k)
+        te.wait_ge(S.kvp, n_k)
+    for b in range(4):
+        te.matmul_mx(bank(b), *stat(b), T.xc[:, 0:256], T.xs[:, 0:256], True, True).then_inc(S["mp%d" % b], 1)
+    n_t = n_lo if is_rank or core == F else n_hi
+    te.wait_ge(S.xtc, n_t)
+    te.wait_ge(S.xtp, n_t)
+    for b in range(4):
+        te.matmul_mx(bank(4 + b), *stat(b), T.xc[:, 256:512], T.xs[:, 256:512], True, True).then_inc(S["ms%d" % b], 1)
+
+    for b in (0, 2):
+        v.wait_ge(S["mp%d" % b], 1)
+        v.tensor_copy(cut(T.pp, b), bank(b)).then_inc(S["cp%d" % b], 1)
+    a.wait_ge(S.ofs, 1)
+    for o in (1, 3):
+        a.wait_ge(S["mp%d" % o], 1)
+        a.activation(cut(T.pp, o), bank(o), copy).then_inc(S["cp%d" % o], 1)
+        for b in (o - 1, o):
+            a.wait_ge(S["cp%d" % b], 1)
+            a.activation(cut(T.pg, b), cut(T.pp, b).indirect(T.off[:, 16 * b:16 * b + 16]), copy).then_inc(S["ga%d" % b], 1)
+    for b in range(4):
+        v.wait_ge(S["ms%d" % b], 1)
+        v.wait_ge(S["ga%d" % b], 1)
+        v.tensor_tensor(T.hh[:, b:1024:4], bank(4 + b), cut(T.pg, b), add).then_inc(S["ad%d" % b], 1)
+        v.wait_ge(S["ad%d" % b], 1)
+        v.tensor_scalar(T.hh[:, b:1024:4], T.hh[:, b:1024:4], 0.0, 0.03125, mx, mult).then_inc(S.clp, 1)
+    v.wait_ge(S.clp, 4)
+    v.quantize_mx(T.kc[:, 0:256], T.ks[:, 0:256], T.hh[:, 0:1024]).then_inc(S.qa, 1)
+
+    A0 = 256 * srank
+    s = S["av%d" % srank]
+    if is_rank:
+        g.wait_ge(S.qa, 1)
+        send(tr(HI, s, code(T.kc, 128, 384), [(oth, code(T.lc, A0, A0 + 256))]))
+        send(tr(HI, s, T.ks[:, 128:384], [(oth, T.ls[:, A0:A0 + 256])]))
+    else:
+        g.wait_ge(S.kvc, n_k)
+        send(tr(LO, s, code(T.kc, 256, 384), [(own, code(T.lc, A0 + 128, A0 + 256))]),
+             tr(HI, s, code(T.kc, 256, 384), [(oth, code(T.lc, A0 + 128, A0 + 256))]))
+        g.wait_ge(S.kvp, n_k)
+        send(tr(LO, s, T.ks[:, 256:384], [(own, T.ls[:, A0 + 128:A0 + 256])]),
+             tr(HI, s, T.ks[:, 256:384], [(oth, T.ls[:, A0 + 128:A0 + 256])]))
+        g.wait_ge(S.qa, 1)
+        send(tr(LO, s, code(T.kc, 0, 128), [(own, code(T.lc, A0, A0 + 128))]),
+             tr(HI, s, code(T.kc, 128, 256), [(oth, code(T.lc, A0, A0 + 128))]))
+        send(tr(LO, s, T.ks[:, 0:128], [(own, T.ls[:, A0:A0 + 128])]),
+             tr(HI, s, T.ks[:, 128:256], [(oth, T.ls[:, A0:A0 + 128])]))
+
+    if is_rank:
+        y = T.ps[:, 0:128]
+        te.wait_ge(S.qa, 1)
+        te.wait_ge(S.zvv, 1)
+        te.matmul_mx(y, T.kc[:, 256:384], T.ks[:, 256:384], T.kc[:, 0:128], T.ks[:, 0:128], True, False)
+        order = [oth] + [rank_at(me - k, e) for k in (1, 2, 3) for e in (d, 1 - d)]
+        for i, r in enumerate(order):
+            k = T.rank_of(r)
+            te.wait_ge(S["av%d" % k], 2 * n_hi if r == oth else 4 * n_lo if topo.die(r) == d else 4 * n_hi)
+            c, last = 256 * k, i == len(order) - 1
+            m = te.matmul_mx(y, T.lc[:, c + 128:c + 256], T.ls[:, c + 128:c + 256], T.lc[:, c:c + 128], T.ls[:, c:c + 128],
+                             False, last)
+        m.then_inc(S.yd, 1)
+        v.wait_ge(S.yd, 1)
+        v.tensor_copy(T.yo[:], y).then_inc(S.yc, 1)
+        g.sync.wait_ge(S.yc, 1)
+        g.sync.dma_start(T.y[:], T.yo[:]).then_inc(S.yst, 16)
+        g.sync.wait_ge(S.yst, 16)
+    g.wait_ge(S.sent, sent[0])

@@ -25,9 +25,11 @@ SCRATCH = {
     "yo": ("sbuf", [128, 128], "float32"),
     "ps": ("psum", [128, 4096], "float32"),
 }
+PIECES = {"h1": (384, 640), "pk": (384, 896), "h2": (640, 896), "vc": (256, 384), "vp": (256, 384)}
 SEMAPHORES = (["lkp", "lqp", "lqx", "lrt", "lvv", "lk0", "lk1", "ckp", "cqp", "zqx", "zrt", "zvv", "zk0", "zk1",
-               "akp", "aqo", "aqt", "xoc", "xop", "xtc", "xtp", "kvc", "kvp", "fwc", "fwp", "sent",
+               "akp", "aqo", "aqt", "xrc", "xrp", "xtc", "xtp", "xac", "xap", "xbc", "xbp", "sent",
                "dl", "ofs", "clp", "qa", "yd", "yc", "yst"]
+              + ["%s%s" % (n, w) for n in "kf" for w in PIECES]
               + ["%s%d" % (n, b) for n in ("mp", "ms", "cp", "ga", "ad") for b in range(4)]
               + ["av%d" % s for s in range(8)])
 
@@ -52,8 +54,7 @@ def rank_program(g, core, T, topo):
     own, oth = rank_at(me, d), rank_at(me, 1 - d)
     F, G, H = helpers(own)
     oF, oG, oH = helpers(oth)
-    far = rank_at(me + 1, d)
-    lo = topo.engines(core, far)
+    lo = topo.engines(core, rank_at(me + 1, d))
     near = topo.engines(core, own if core != own else oth)
     hi = [e for e in near if e not in lo]
     LO, HI, ALL = [sum(1 << e for e in es) for es in (lo, hi, near)]
@@ -61,6 +62,7 @@ def rank_program(g, core, T, topo):
     is_rank = core == own
     src = own if is_rank else rank_at(me - {H: 1, G: 2, F: 3}[core], d)
     srank = T.rank_of(src)
+    one, two, three = [helpers(rank_at(me + k, d))[3 - k] for k in (1, 2, 3)]
     sent = [0]
 
     def tr(mask, sem, src_ap, dests):
@@ -77,29 +79,33 @@ def rank_program(g, core, T, topo):
     def code(t, i, j):
         return t[:, i:j].bitcast(dt.uint8)
 
+    def piece(t_c, t_s, w, o=0):
+        i, j = PIECES[w]
+        return t_s[:, i - o:j - o] if w in ("pk", "vp") else code(t_c, i - o, j - o)
+
     sub, add, mx, mn, mult = AluOpType.subtract, AluOpType.add, AluOpType.max, AluOpType.min, AluOpType.mult
     copy = ActivationFunctionType.Copy
     v, a, te = g.vector, g.scalar, g.tensor
+    q_own, q_oth = T.qp16[:, 0:8], T.qp16[:, 8:16]
 
     if is_rank:
-        g.scalar.dma_start(T.kpi[:], T.kp[:]).then_inc(S.lkp, 16)
-        g.sync.dma_start(T.xb[:, 1024:1536], T.qx[:]).then_inc(S.lqx, 16)
-        g.scalar.dma_start(T.xb[:, 0:1024], T.rt[:]).then_inc(S.lrt, 16)
-        g.sync.dma_start(T.kb[:, 512:1536], T.ky[:, 0:1024]).then_inc(S.lk0, 16)
+        a.dma_start(T.kpi[:], T.kp[:]).then_inc(S.lkp, 16)
         for k in range(8):
-            q = g.sync if k % 2 else g.scalar
-            q.dma_start(T.qpi[16 * k:16 * k + 16, :], T.qp[:]).then_inc(S.lqp, 16)
-        g.scalar.dma_start(T.kb[:, 1536:2560], T.ky[:, 1024:2048]).then_inc(S.lk1, 16)
+            (a if k % 2 else g.sync).dma_start(T.qpi[16 * k:16 * k + 16, :], T.qp[:]).then_inc(S.lqp, 16)
+        g.sync.dma_start(T.xb[:, 1024:1536], T.qx[:]).then_inc(S.lqx, 16)
+        a.dma_start(T.xb[:, 0:1024], T.rt[:]).then_inc(S.lrt, 16)
+        g.sync.dma_start(T.kb[:, 512:1536], T.ky[:, 0:1024]).then_inc(S.lk0, 16)
+        a.dma_start(T.kb[:, 1536:2560], T.ky[:, 1024:2048]).then_inc(S.lk1, 16)
         g.sync.dma_start(T.kb[:, 0:512], T.vv[:]).then_inc(S.lvv, 16)
 
         v.wait_ge(S.lkp, 16)
         v.tensor_copy(T.kpf[:], T.kpi[:]).then_inc(S.ckp, 1)
+        v.wait_ge(S.lqp, 128)
+        v.tensor_copy(q_own, T.qpi[:]).then_inc(S.cqp, 1)
         v.wait_ge(S.lqx, 16)
         v.quantize_mx(T.xc[:, 256:384], T.xs[:, 256:384], T.xb[:, 1024:1536]).then_inc(S.zqx, 1)
         v.wait_ge(S.lrt, 16)
         v.quantize_mx(T.xc[:, 0:256], T.xs[:, 0:256], T.xb[:, 0:1024]).then_inc(S.zrt, 1)
-        v.wait_ge(S.lqp, 128)
-        v.tensor_copy(T.qp16[:, 0:8], T.qpi[:]).then_inc(S.cqp, 1)
         v.wait_ge(S.lk0, 16)
         v.quantize_mx(T.kc[:, 384:640], T.ks[:, 384:640], T.kb[:, 512:1536]).then_inc(S.zk0, 1)
         v.wait_ge(S.lk1, 16)
@@ -107,50 +113,50 @@ def rank_program(g, core, T, topo):
         v.wait_ge(S.lvv, 16)
         v.quantize_mx(T.kc[:, 256:384], T.ks[:, 256:384], T.kb[:, 0:512]).then_inc(S.zvv, 1)
 
-        one, two, three = helpers(rank_at(me + 1, d))[2], helpers(rank_at(me + 2, d))[1], helpers(rank_at(me + 3, d))[0]
         g.wait_ge(S.ckp, 1)
-        send(tr(LO, S.akp, T.kpf[:], [(one, T.kpf[:]), (two, T.kpf[:]), (three, T.kpf[:])]))
+        g.wait_ge(S.cqp, 1)
+        send(tr(LO, S.akp, T.kpf[:], [(c, T.kpf[:]) for c in (one, two, three)]),
+             tr(HI, S.aqo, q_own, [(c, q_own) for c in (F, G, H)]))
         g.wait_ge(S.zqx, 1)
         g.wait_ge(S.zrt, 1)
-        send(tr(ALL, S.xoc, code(T.xc, 0, 384), [(F, code(T.xc, 0, 384))]))
-        send(tr(ALL, S.xop, T.xs[:, 0:384], [(F, T.xs[:, 0:384])]))
-        g.wait_ge(S.cqp, 1)
-        send(tr(HI, S.aqo, T.qp16[:, 0:8], [(F, T.qp16[:, 0:8])]))
-        g.wait_ge(S.zk0, 1)
-        g.wait_ge(S.zk1, 1)
-        g.wait_ge(S.zvv, 1)
-        send(tr(LO, S.kvc, code(T.kc, 256, 896), [(one, code(T.kc, 256, 896)), (two, code(T.kc, 256, 896))]),
-             tr(HI, S.fwc, code(T.kc, 256, 896), [(G, code(T.fc, 0, 640))]))
-        send(tr(LO, S.kvp, T.ks[:, 256:896], [(one, T.ks[:, 256:896]), (two, T.ks[:, 256:896])]),
-             tr(HI, S.fwp, T.ks[:, 256:896], [(G, T.fs[:, 0:640])]))
-    elif core == F:
-        g.wait_ge(S.xoc, n_all)
-        send(tr(LO, S.xtc, code(T.xc, 256, 384), [(c, code(T.xc, 384, 512)) for c in (oth, oF)]),
-             tr(HI, S.xtc, code(T.xc, 256, 384), [(c, code(T.xc, 384, 512)) for c in (oG, oH)]))
-        g.wait_ge(S.xop, n_all)
-        send(tr(LO, S.xtp, T.xs[:, 256:384], [(c, T.xs[:, 384:512]) for c in (oth, oF)]),
-             tr(HI, S.xtp, T.xs[:, 256:384], [(c, T.xs[:, 384:512]) for c in (oG, oH)]))
+        send(tr(ALL, S.xrc, code(T.xc, 0, 384), [(F, code(T.xc, 0, 384))]))
+        send(tr(ALL, S.xrp, T.xs[:, 0:384], [(F, T.xs[:, 0:384])]))
+        ready = {"h1": "zk0", "pk": "zk1", "vc": "zvv"}
+        for w in PIECES:
+            if w in ready:
+                g.wait_ge(S[ready[w]], 1)
+            p = piece(T.kc, T.ks, w)
+            send(tr(LO, S["k" + w], p, [(one, p), (two, p)]), tr(HI, S["f" + w], p, [(G, piece(T.fc, T.fs, w, 256))]))
+    else:
         g.wait_ge(S.aqo, n_hi)
-        send(tr(LO, S.aqo, T.qp16[:, 0:8], [(c, T.qp16[:, 0:8]) for c in (G, H)]),
-             tr(HI, S.aqt, T.qp16[:, 0:8], [(c, T.qp16[:, 8:16]) for c in (oth, oF, oG, oH)]))
-        send(tr(LO, S.xoc, code(T.xc, 0, 384), [(H, code(T.xc, 0, 384))]),
-             tr(HI, S.xoc, code(T.xc, 0, 384), [(G, code(T.xc, 0, 384))]))
-        send(tr(LO, S.xop, T.xs[:, 0:384], [(H, T.xs[:, 0:384])]),
-             tr(HI, S.xop, T.xs[:, 0:384], [(G, T.xs[:, 0:384])]))
-    elif core == G:
-        three = helpers(rank_at(me + 3, d))[0]
-        g.wait_ge(S.fwc, n_hi)
-        send(tr(LO, S.kvc, code(T.fc, 0, 640), [(three, code(T.kc, 256, 896))]))
-        g.wait_ge(S.fwp, n_hi)
-        send(tr(LO, S.kvp, T.fs[:, 0:640], [(three, T.ks[:, 256:896])]))
+        if core == F:
+            send(tr(LO, S.aqt, q_own, [(oF, q_oth), (oG, q_oth)]), tr(HI, S.aqt, q_own, [(oH, q_oth), (oth, q_oth)]))
+            x_own, x_oth = code(T.xc, 256, 384), code(T.xc, 384, 512)
+            s_own, s_oth = T.xs[:, 256:384], T.xs[:, 384:512]
+            g.wait_ge(S.xrc, n_all)
+            send(tr(LO, S.xtc, x_own, [(oF, x_oth)]), tr(HI, S.xtc, x_own, [(oth, x_oth)]))
+            g.wait_ge(S.xrp, n_all)
+            send(tr(LO, S.xtp, s_own, [(oF, s_oth)]), tr(HI, S.xtp, s_own, [(oth, s_oth)]))
+            p = code(T.xc, 0, 384)
+            send(tr(LO, S.xac, p, [(H, p)]), tr(HI, S.xac, p, [(G, p)]))
+            p = T.xs[:, 0:384]
+            send(tr(LO, S.xap, p, [(H, p)]), tr(HI, S.xap, p, [(G, p)]))
+            g.wait_ge(S.xtc, n_lo)
+            send(tr(LO, S.xbc, x_oth, [(H, x_oth)]), tr(HI, S.xbc, x_oth, [(G, x_oth)]))
+            g.wait_ge(S.xtp, n_lo)
+            send(tr(LO, S.xbp, s_oth, [(H, s_oth)]), tr(HI, S.xbp, s_oth, [(G, s_oth)]))
+        if core == G:
+            for w in PIECES:
+                g.wait_ge(S["f" + w], n_hi)
+                send(tr(LO, S["k" + w], piece(T.fc, T.fs, w, 256), [(three, piece(T.kc, T.ks, w))]))
 
     if is_rank:
         v.wait_ge(S.ckp, 1)
         v.wait_ge(S.cqp, 1)
     else:
         v.wait_ge(S.akp, n_lo)
-        v.wait_ge(S.aqo, n_hi if core == F else n_lo)
-    v.wait_ge(S.aqt, n_hi)
+        v.wait_ge(S.aqo, n_hi)
+    v.wait_ge(S.aqt, n_lo)
     for b in range(4):
         v.tensor_scalar(T.dd[:, 16 * b:16 * b + 16], T.qp16[:], T.kpf[:, b:b + 1], -128.0, sub, mx).then_inc(S.dl, 1)
     v.wait_ge(S.dl, 4)
@@ -166,33 +172,35 @@ def rank_program(g, core, T, topo):
         return T.ps[:, 512 * b:512 * b + 256]
 
     if is_rank:
-        te.wait_ge(S.zrt, 1)
-        te.wait_ge(S.zqx, 1)
-        te.wait_ge(S.zk0, 1)
-        te.wait_ge(S.zk1, 1)
+        x_sems = [(S.zrt, 1), (S.zqx, 1)]
+        t_sems = [(S.xtc, n_hi), (S.xtp, n_hi)]
+    elif core == F:
+        x_sems = [(S.xrc, n_all), (S.xrp, n_all)]
+        t_sems = [(S.xtc, n_lo), (S.xtp, n_lo)]
     else:
-        n_x = n_all if core == F else n_lo if core == H else n_hi
-        n_k = n_lo
-        te.wait_ge(S.xoc, n_x)
-        te.wait_ge(S.xop, n_x)
-        te.wait_ge(S.kvc, n_k)
-        te.wait_ge(S.kvp, n_k)
-    for b in range(4):
-        te.matmul_mx(bank(b), *stat(b), T.xc[:, 0:256], T.xs[:, 0:256], True, True).then_inc(S["mp%d" % b], 1)
-    n_t = n_lo if is_rank or core == F else n_hi
-    te.wait_ge(S.xtc, n_t)
-    te.wait_ge(S.xtp, n_t)
-    for b in range(4):
-        te.matmul_mx(bank(4 + b), *stat(b), T.xc[:, 256:512], T.xs[:, 256:512], True, True).then_inc(S["ms%d" % b], 1)
+        x_sems = [(S.xac, n_hi), (S.xap, n_hi)]
+        t_sems = [(S.xbc, n_hi), (S.xbp, n_hi)]
+    for h in (0, 1):
+        k_sems = [(S["zk%d" % h], 1)] if is_rank else [(S["kh%d" % (h + 1)], n_lo), (S.kpk, n_lo)]
+        for sem, val in k_sems + x_sems * (1 - h):
+            te.wait_ge(sem, val)
+        for b in (2 * h, 2 * h + 1):
+            te.matmul_mx(bank(b), *stat(b), T.xc[:, 0:256], T.xs[:, 0:256], True, True).then_inc(S["mp%d" % b], 1)
+        for sem, val in t_sems * (1 - h):
+            te.wait_ge(sem, val)
+        for b in (2 * h, 2 * h + 1):
+            te.matmul_mx(bank(4 + b), *stat(b), T.xc[:, 256:512], T.xs[:, 256:512], True, True).then_inc(S["ms%d" % b], 1)
 
-    for b in (0, 2):
+    for b in (0, 1):
         v.wait_ge(S["mp%d" % b], 1)
         v.tensor_copy(cut(T.pp, b), bank(b)).then_inc(S["cp%d" % b], 1)
     a.wait_ge(S.ofs, 1)
-    for o in (1, 3):
-        a.wait_ge(S["mp%d" % o], 1)
-        a.activation(cut(T.pp, o), bank(o), copy).then_inc(S["cp%d" % o], 1)
-        for b in (o - 1, o):
+    for h in (0, 1):
+        if h:
+            for b in (2, 3):
+                a.wait_ge(S["mp%d" % b], 1)
+                a.activation(cut(T.pp, b), bank(b), copy).then_inc(S["cp%d" % b], 1)
+        for b in (2 * h, 2 * h + 1):
             a.wait_ge(S["cp%d" % b], 1)
             a.activation(cut(T.pg, b), cut(T.pp, b).indirect(T.off[:, 16 * b:16 * b + 16]), copy).then_inc(S["ga%d" % b], 1)
     for b in range(4):
@@ -211,17 +219,15 @@ def rank_program(g, core, T, topo):
         send(tr(HI, s, code(T.kc, 128, 384), [(oth, code(T.lc, A0, A0 + 256))]))
         send(tr(HI, s, T.ks[:, 128:384], [(oth, T.ls[:, A0:A0 + 256])]))
     else:
-        g.wait_ge(S.kvc, n_k)
-        send(tr(LO, s, code(T.kc, 256, 384), [(own, code(T.lc, A0 + 128, A0 + 256))]),
-             tr(HI, s, code(T.kc, 256, 384), [(oth, code(T.lc, A0 + 128, A0 + 256))]))
-        g.wait_ge(S.kvp, n_k)
-        send(tr(LO, s, T.ks[:, 256:384], [(own, T.ls[:, A0 + 128:A0 + 256])]),
-             tr(HI, s, T.ks[:, 256:384], [(oth, T.ls[:, A0 + 128:A0 + 256])]))
+        def both(own_ap, oth_ap, land):
+            send(tr(LO, s, own_ap, [(own, land)]), tr(HI, s, oth_ap, [(oth, land)]))
+        g.wait_ge(S.kvc, n_lo)
+        both(code(T.kc, 256, 384), code(T.kc, 256, 384), code(T.lc, A0 + 128, A0 + 256))
+        g.wait_ge(S.kvp, n_lo)
+        both(T.ks[:, 256:384], T.ks[:, 256:384], T.ls[:, A0 + 128:A0 + 256])
         g.wait_ge(S.qa, 1)
-        send(tr(LO, s, code(T.kc, 0, 128), [(own, code(T.lc, A0, A0 + 128))]),
-             tr(HI, s, code(T.kc, 128, 256), [(oth, code(T.lc, A0, A0 + 128))]))
-        send(tr(LO, s, T.ks[:, 0:128], [(own, T.ls[:, A0:A0 + 128])]),
-             tr(HI, s, T.ks[:, 128:256], [(oth, T.ls[:, A0:A0 + 128])]))
+        both(code(T.kc, 0, 128), code(T.kc, 128, 256), code(T.lc, A0, A0 + 128))
+        both(T.ks[:, 0:128], T.ks[:, 128:256], T.ls[:, A0:A0 + 128])
 
     if is_rank:
         y = T.ps[:, 0:128]

@@ -5,33 +5,34 @@ C4, U8 = "float8_e4m3fn_x4", "uint8"
 SCRATCH = {
     "xb": ("sbuf", [128, 1536], "bfloat16"),
     "kb": ("sbuf", [128, 2560], "bfloat16"),
-    "xc": ("sbuf", [128, 512], C4),
-    "xs": ("sbuf", [128, 512], U8),
-    "kc": ("sbuf", [128, 896], C4),
-    "ks": ("sbuf", [128, 896], U8),
-    "fc": ("sbuf", [128, 640], C4),
-    "fs": ("sbuf", [128, 640], U8),
+    "xc": ("sbuf", [128, 768], C4),
+    "xs": ("sbuf", [128, 768], U8),
+    "kc": ("sbuf", [128, 1152], C4),
+    "ks": ("sbuf", [128, 1152], U8),
     "lc": ("sbuf", [128, 2048], C4),
     "ls": ("sbuf", [128, 2048], U8),
     "qpi": ("sbuf", [128, 8], "int32"),
-    "qp16": ("sbuf", [128, 16], "uint16"),
+    "qp16": ("sbuf", [128, 32], "uint16"),
     "kpi": ("sbuf", [128, 4], "int32"),
     "kpf": ("sbuf", [128, 4], "float32"),
-    "dd": ("sbuf", [128, 64], "float32"),
-    "off": ("sbuf", [128, 64], "uint16"),
+    "dd": ("sbuf", [128, 128], "float32"),
+    "off": ("sbuf", [128, 128], "uint16"),
     "pp": ("sbuf", [128, 1024], "float32"),
-    "pg": ("sbuf", [128, 1024], "float32"),
-    "hh": ("sbuf", [128, 1024], "bfloat16"),
+    "pg": ("sbuf", [128, 2048], "float32"),
+    "hh": ("sbuf", [128, 2048], "bfloat16"),
     "yo": ("sbuf", [128, 128], "float32"),
     "ps": ("psum", [128, 4096], "float32"),
 }
-PIECES = {"h1": (384, 640), "pk": (384, 896), "h2": (640, 896), "vc": (256, 384), "vp": (256, 384)}
+PIECES = {"h1": (640, 896), "pk": (640, 1152), "h2": (896, 1152)}
 SEMAPHORES = (["lkp", "lqp", "lqx", "lrt", "lvv", "lk0", "lk1", "ckp", "cqp", "zqx", "zrt", "zvv", "zk0", "zk1",
-               "akp", "aqo", "aqt", "xrc", "xrp", "xtc", "xtp", "xac", "xap", "xbc", "xbp", "sent",
-               "dl", "ofs", "clp", "qa", "yd", "yc", "yst"]
-              + ["%s%s" % (n, w) for n in "kf" for w in PIECES]
-              + ["%s%d" % (n, b) for n in ("mp", "ms", "cp", "ga", "ad") for b in range(4)]
-              + ["av%d" % s for s in range(8)])
+               "akp", "aqo", "aqt", "aqf", "xoc", "xop", "xac", "xap", "xtc", "xtp", "xfc", "xfp",
+               "vfc", "vfp", "vwc", "vwp", "sent", "yd", "yc", "yst"]
+              + ["k" + w for w in PIECES]
+              + ["%s%d" % (n, b) for n in ("mp", "cp") for b in range(4)]
+              + ["%s%d%d" % (n, q, b) for n in ("ms", "ga", "ad") for q in (0, 1) for b in range(4)]
+              + ["%s%d" % (n, b) for n in ("gb", "ae") for b in (2, 3)]
+              + ["%s%d" % (n, q) for n in ("dl", "ofs", "clp", "qa", "qb") for q in (0, 1)]
+              + ["%s%d" % (n, s) for n in ("av", "vs") for s in range(8)])
 
 
 def rank_program(g, core, T, topo):
@@ -52,17 +53,19 @@ def rank_program(g, core, T, topo):
 
     me, d = chips.index(topo.chip(core)), topo.die(core)
     own, oth = rank_at(me, d), rank_at(me, 1 - d)
-    F, G, H = helpers(own)
-    oF, oG, oH = helpers(oth)
+    F, G, W = helpers(own)
+    oW = helpers(oth)[2]
     lo = topo.engines(core, rank_at(me + 1, d))
     near = topo.engines(core, own if core != own else oth)
     hi = [e for e in near if e not in lo]
-    LO, HI, ALL = [sum(1 << e for e in es) for es in (lo, hi, near)]
-    n_lo, n_hi, n_all = len(lo), len(hi), len(near)
+    LO, HI, ALL, L0, L1 = [sum(1 << e for e in es) for es in (lo, hi, near, lo[:len(lo) // 2], lo[len(lo) // 2:])]
+    n_lo, n_hi, n_all, n_l2 = len(lo), len(hi), len(near), len(lo) // 2
     is_rank = core == own
-    src = own if is_rank else rank_at(me - {H: 1, G: 2, F: 3}[core], d)
+    src = rank_at(me - 1, d) if core == W else own
     srank = T.rank_of(src)
-    one, two, three = [helpers(rank_at(me + k, d))[3 - k] for k in (1, 2, 3)]
+    r1, r2, r3 = [[rank_at(me + k, e) for e in (d, 1 - d)] for k in (1, 2, 3)]
+    f1, w1 = helpers(r1[0])[0], helpers(r1[0])[2]
+    far = [helpers(r)[1] for r in r2]
     sent = [0]
 
     def tr(mask, sem, src_ap, dests):
@@ -76,17 +79,24 @@ def rank_program(g, core, T, topo):
     def send(*ts):
         g.remote_dma_fused(list(ts), local_sem=S.sent)
 
-    def code(t, i, j):
-        return t[:, i:j].bitcast(dt.uint8)
+    def cols(x, i, j, w):
+        return T[x + "c"][:, i:j].bitcast(dt.uint8) if w == "c" else T[x + "s"][:, i:j]
 
-    def piece(t_c, t_s, w, o=0):
-        i, j = PIECES[w]
-        return t_s[:, i - o:j - o] if w in ("pk", "vp") else code(t_c, i - o, j - o)
+    def land(s, part):
+        c = 256 * s + 128 * part
+        return c, c + 128
 
     sub, add, mx, mn, mult = AluOpType.subtract, AluOpType.add, AluOpType.max, AluOpType.min, AluOpType.mult
     copy = ActivationFunctionType.Copy
     v, a, te = g.vector, g.scalar, g.tensor
-    q_own, q_oth = T.qp16[:, 0:8], T.qp16[:, 8:16]
+    q4 = [T.qp16[:, 8 * i:8 * i + 8] for i in range(4)]
+    X = [(256 + 128 * i, 384 + 128 * i) for i in range(4)]
+    V0, V1 = 512, 640
+    vs, av = S["vs%d" % srank], S["av%d" % srank]
+
+    def give_v(mask, w, to):
+        p, at = cols("k", V0, V1, w), cols("l", *land(srank, 1), w)
+        send(tr(mask, vs, p, [(c, at) for c in to]))
 
     if is_rank:
         a.dma_start(T.kpi[:], T.kp[:]).then_inc(S.lkp, 16)
@@ -98,149 +108,244 @@ def rank_program(g, core, T, topo):
         a.dma_start(T.kb[:, 1536:2560], T.ky[:, 1024:2048]).then_inc(S.lk1, 16)
         g.sync.dma_start(T.kb[:, 0:512], T.vv[:]).then_inc(S.lvv, 16)
 
+        v.wait_ge(S.lqp, 128)
+        v.tensor_copy(q4[0], T.qpi[:]).then_inc(S.cqp, 1)
         v.wait_ge(S.lkp, 16)
         v.tensor_copy(T.kpf[:], T.kpi[:]).then_inc(S.ckp, 1)
-        v.wait_ge(S.lqp, 128)
-        v.tensor_copy(q_own, T.qpi[:]).then_inc(S.cqp, 1)
         v.wait_ge(S.lqx, 16)
         v.quantize_mx(T.xc[:, 256:384], T.xs[:, 256:384], T.xb[:, 1024:1536]).then_inc(S.zqx, 1)
         v.wait_ge(S.lrt, 16)
         v.quantize_mx(T.xc[:, 0:256], T.xs[:, 0:256], T.xb[:, 0:1024]).then_inc(S.zrt, 1)
         v.wait_ge(S.lk0, 16)
-        v.quantize_mx(T.kc[:, 384:640], T.ks[:, 384:640], T.kb[:, 512:1536]).then_inc(S.zk0, 1)
+        v.quantize_mx(T.kc[:, 640:896], T.ks[:, 640:896], T.kb[:, 512:1536]).then_inc(S.zk0, 1)
         v.wait_ge(S.lk1, 16)
-        v.quantize_mx(T.kc[:, 640:896], T.ks[:, 640:896], T.kb[:, 1536:2560]).then_inc(S.zk1, 1)
+        v.quantize_mx(T.kc[:, 896:1152], T.ks[:, 896:1152], T.kb[:, 1536:2560]).then_inc(S.zk1, 1)
         v.wait_ge(S.lvv, 16)
-        v.quantize_mx(T.kc[:, 256:384], T.ks[:, 256:384], T.kb[:, 0:512]).then_inc(S.zvv, 1)
+        v.quantize_mx(T.kc[:, V0:V1], T.ks[:, V0:V1], T.kb[:, 0:512]).then_inc(S.zvv, 1)
 
-        g.wait_ge(S.ckp, 1)
+        g.wait_ge(S.lkp, 16)
+        send(tr(LO, S.akp, T.kpi[:], [(w1, T.kpi[:])]), tr(HI, S.akp, T.kpi[:], [(G, T.kpi[:])]))
         g.wait_ge(S.cqp, 1)
-        send(tr(LO, S.akp, T.kpf[:], [(c, T.kpf[:]) for c in (one, two, three)]),
-             tr(HI, S.aqo, q_own, [(c, q_own) for c in (F, G, H)]))
+        send(tr(LO, S.aqo, q4[0], [(f1, q4[0])]), tr(HI, S.aqo, q4[0], [(G, q4[0]), (W, q4[0])]))
         g.wait_ge(S.zqx, 1)
+        for w in "cp":
+            p = cols("x", *X[0], w)
+            send(tr(LO, S["xo" + w], p, [(f1, p)]), tr(HI, S["xo" + w], p, [(W, p)]))
         g.wait_ge(S.zrt, 1)
-        send(tr(ALL, S.xrc, code(T.xc, 0, 384), [(F, code(T.xc, 0, 384))]))
-        send(tr(ALL, S.xrp, T.xs[:, 0:384], [(F, T.xs[:, 0:384])]))
-        ready = {"h1": "zk0", "pk": "zk1", "vc": "zvv"}
+        for w in "cp":
+            p = cols("x", 0, 256, w)
+            send(tr(ALL, S["xa" + w], p, [(G, p)]))
         for w in PIECES:
-            if w in ready:
-                g.wait_ge(S[ready[w]], 1)
-            p = piece(T.kc, T.ks, w)
-            send(tr(LO, S["k" + w], p, [(one, p), (two, p)]), tr(HI, S["f" + w], p, [(G, piece(T.fc, T.fs, w, 256))]))
-    else:
-        g.wait_ge(S.aqo, n_hi)
-        if core == F:
-            send(tr(LO, S.aqt, q_own, [(oF, q_oth), (oG, q_oth)]), tr(HI, S.aqt, q_own, [(oH, q_oth), (oth, q_oth)]))
-            x_own, x_oth = code(T.xc, 256, 384), code(T.xc, 384, 512)
-            s_own, s_oth = T.xs[:, 256:384], T.xs[:, 384:512]
-            g.wait_ge(S.xrc, n_all)
-            send(tr(LO, S.xtc, x_own, [(oF, x_oth)]), tr(HI, S.xtc, x_own, [(oth, x_oth)]))
-            g.wait_ge(S.xrp, n_all)
-            send(tr(LO, S.xtp, s_own, [(oF, s_oth)]), tr(HI, S.xtp, s_own, [(oth, s_oth)]))
-            p = code(T.xc, 0, 384)
-            send(tr(LO, S.xac, p, [(H, p)]), tr(HI, S.xac, p, [(G, p)]))
-            p = T.xs[:, 0:384]
-            send(tr(LO, S.xap, p, [(H, p)]), tr(HI, S.xap, p, [(G, p)]))
-            g.wait_ge(S.xtc, n_lo)
-            send(tr(LO, S.xbc, x_oth, [(H, x_oth)]), tr(HI, S.xbc, x_oth, [(G, x_oth)]))
-            g.wait_ge(S.xtp, n_lo)
-            send(tr(LO, S.xbp, s_oth, [(H, s_oth)]), tr(HI, S.xbp, s_oth, [(G, s_oth)]))
-        if core == G:
-            for w in PIECES:
-                g.wait_ge(S["f" + w], n_hi)
-                send(tr(LO, S["k" + w], piece(T.fc, T.fs, w, 256), [(three, piece(T.kc, T.ks, w))]))
+            if w != "h2":
+                g.wait_ge(S.zk0 if w == "h1" else S.zk1, 1)
+            p = cols("k", *PIECES[w], "p" if w == "pk" else "c")
+            send(tr(LO, S["k" + w], p, [(w1, p)]), tr(HI, S["k" + w], p, [(G, p)]))
+        g.wait_ge(S.zvv, 1)
+        for w in "cp":
+            p = cols("k", V0, V1, w)
+            send(tr(LO, S["vw" + w], p, [(w1, p)]), tr(HI, S["vf" + w], p, [(F, p), (G, p)]))
+        for w in "cp":
+            give_v(HI, w, [oth])
 
-    if is_rank:
-        v.wait_ge(S.ckp, 1)
-        v.wait_ge(S.cqp, 1)
-    else:
-        v.wait_ge(S.akp, n_lo)
-        v.wait_ge(S.aqo, n_hi)
-    v.wait_ge(S.aqt, n_lo)
-    for b in range(4):
-        v.tensor_scalar(T.dd[:, 16 * b:16 * b + 16], T.qp16[:], T.kpf[:, b:b + 1], -128.0, sub, mx).then_inc(S.dl, 1)
-    v.wait_ge(S.dl, 4)
-    v.tensor_scalar(T.off[:], T.dd[:], 127.0, 128.0, mn, add).then_inc(S.ofs, 1)
+    elif core == F:
+        g.wait_ge(S.aqo, n_lo)
+        send(tr(LO, S.aqf, q4[0], [(own, q4[2])]), tr(HI, S.aqf, q4[0], [(oth, q4[3])]))
+        for w in "cp":
+            g.wait_ge(S["xo" + w], n_lo)
+            p = cols("x", *X[0], w)
+            send(tr(LO, S["xf" + w], p, [(own, cols("x", *X[2], w))]), tr(HI, S["xf" + w], p, [(oth, cols("x", *X[3], w))]))
+        for w in "cp":
+            g.wait_ge(S["vf" + w], n_hi)
+            give_v(LO, w, r3)
+        g.wait_ge(S.sent, sent[0])
+        return
+    elif core == G:
+        g.wait_ge(S.aqo, n_hi)
+        send(tr(LO, S.aqf, q4[0], [(far[0], q4[2]), (far[1], q4[3])]))
+        for w in "cp":
+            g.wait_ge(S["xa" + w], n_all)
+            p = cols("x", 0, 256, w)
+            send(tr(LO, S["xa" + w], p, [(W, p)]))
+        for w in "cp":
+            g.wait_ge(S["vf" + w], n_hi)
+            give_v(LO, w, r2)
+    elif core == W:
+        g.wait_ge(S.aqo, n_hi)
+        send(tr(LO, S.aqt, q4[0], [(oW, q4[1])]), tr(HI, S.aqt, q4[0], [(oth, q4[1])]))
+        for w in "cp":
+            g.wait_ge(S["xo" + w], n_hi)
+            p, to = cols("x", *X[0], w), cols("x", *X[1], w)
+            send(tr(LO, S["xf" + w], p, [(far[i], cols("x", *X[2 + i], w)) for i in (0, 1)]),
+                 tr(HI, S["xt" + w], p, [(oW, to), (oth, to)]))
+        for w in "cp":
+            g.wait_ge(S["vw" + w], n_lo)
+            give_v(ALL, w, (own, oth))
+
+    def lists(q):
+        for b in range(4):
+            o = 64 * q + 16 * b
+            v.tensor_scalar(T.dd[:, o:o + 16], T.qp16[:, 16 * q:16 * q + 16], T.kpf[:, b:b + 1], -128.0, sub, mx).then_inc(S["dl%d" % q], 1)
+        v.wait_ge(S["dl%d" % q], 4)
+        v.tensor_scalar(T.off[:, 64 * q:64 * q + 64], T.dd[:, 64 * q:64 * q + 64], 127.0, 128.0, mn, add).then_inc(S["ofs%d" % q], 1)
 
     def stat(b):
-        return T.kc[:, 384 + 128 * b:512 + 128 * b], T.ks[:, 384 + 128 * b:512 + 128 * b]
+        return T.kc[:, 640 + 128 * b:768 + 128 * b], T.ks[:, 640 + 128 * b:768 + 128 * b]
 
-    def cut(t, b):
-        return t[:, 256 * b:256 * b + 256]
+    def bank(b, i=0, w=256):
+        return T.ps[:, 512 * b + i:512 * b + i + w]
 
-    def bank(b):
-        return T.ps[:, 512 * b:512 * b + 256]
+    def sbank(q, b):
+        return b if is_rank and q == 0 else 4 + b
+
+    def product_p(b):
+        te.matmul_mx(bank(b), *stat(b), T.xc[:, 0:256], T.xs[:, 0:256], True, True).then_inc(S["mp%d" % b], 1)
+
+    def product_s(q, b):
+        i = 256 + 256 * q
+        te.matmul_mx(bank(sbank(q, b)), *stat(b), T.xc[:, i:i + 256], T.xs[:, i:i + 256], True, True).then_inc(S["ms%d%d" % (q, b)], 1)
+
+    def copy_p(eng, b):
+        p = T.pp[:, 256 * b:256 * b + 256]
+        eng.wait_ge(S["mp%d" % b], 1)
+        (v.tensor_copy(p, bank(b)) if eng is v else a.activation(p, bank(b), copy)).then_inc(S["cp%d" % b], 1)
+
+    def gather(q, b, i=0, w=256, second=False):
+        o, r = 64 * q + 16 * b + i // 16, 1024 * q + 256 * b + i
+        done = S["gb%d" % b] if second else S["ga%d%d" % (q, b)]
+        a.activation(T.pg[:, r:r + w], T.pp[:, 256 * b:256 * b + 256].indirect(T.off[:, o:o + w // 16]), copy).then_inc(done, 1)
+
+    def finish(q, bs, i=0, w=256, second=False):
+        o = 1024 * q + 4 * i
+        added = {b: S["ae%d" % b] if second else S["ad%d%d" % (q, b)] for b in bs}
+        for b in bs:
+            r = 1024 * q + 256 * b + i
+            v.wait_ge(S["ms%d%d" % (q, b)], 1)
+            v.wait_ge(S["gb%d" % b] if second else S["ga%d%d" % (q, b)], 1)
+            v.tensor_tensor(T.hh[:, o + b:o + 4 * w:4], bank(sbank(q, b), i, w), T.pg[:, r:r + w], add).then_inc(added[b], 1)
+        for b in bs:
+            h = T.hh[:, o + b:o + 4 * w:4]
+            v.wait_ge(added[b], 1)
+            v.tensor_scalar(h, h, 0.0, 0.03125, mx, mult).then_inc(S["clp%d" % q], 1)
+
+    def pack(q, i, w, clipped, name):
+        v.wait_ge(S["clp%d" % q], clipped)
+        k, t = 256 * q + i, 1024 * q + 4 * i
+        v.quantize_mx(T.kc[:, k:k + w], T.ks[:, k:k + w], T.hh[:, t:t + 4 * w]).then_inc(S[name], 1)
+
+    def send_a(name, q, *ts):
+        g.wait_ge(S[name], 1)
+        for w in "cp":
+            to = cols("l", *land(srank, 0), w)
+            send(*[tr(m, av, cols("k", 256 * q + 128 * i, 256 * q + 128 * i + 128, w), [(c, to)]) for i, m, c in ts])
 
     if is_rank:
-        x_sems = [(S.zrt, 1), (S.zqx, 1)]
-        t_sems = [(S.xtc, n_hi), (S.xtp, n_hi)]
-    elif core == F:
-        x_sems = [(S.xrc, n_all), (S.xrp, n_all)]
-        t_sems = [(S.xtc, n_lo), (S.xtp, n_lo)]
-    else:
-        x_sems = [(S.xac, n_hi), (S.xap, n_hi)]
-        t_sems = [(S.xbc, n_hi), (S.xbp, n_hi)]
-    for h in (0, 1):
-        k_sems = [(S["zk%d" % h], 1)] if is_rank else [(S["kh%d" % (h + 1)], n_lo), (S.kpk, n_lo)]
-        for sem, val in k_sems + x_sems * (1 - h):
-            te.wait_ge(sem, val)
-        for b in (2 * h, 2 * h + 1):
-            te.matmul_mx(bank(b), *stat(b), T.xc[:, 0:256], T.xs[:, 0:256], True, True).then_inc(S["mp%d" % b], 1)
-        for sem, val in t_sems * (1 - h):
-            te.wait_ge(sem, val)
-        for b in (2 * h, 2 * h + 1):
-            te.matmul_mx(bank(4 + b), *stat(b), T.xc[:, 256:512], T.xs[:, 256:512], True, True).then_inc(S["ms%d" % b], 1)
+        te.wait_ge(S.zrt, 1)
+        te.wait_ge(S.zk0, 1)
+        product_p(0)
+        product_p(1)
+        te.wait_ge(S.zk1, 1)
+        product_p(2)
+        product_p(3)
+        te.wait_ge(S.xfc, n_all)
+        te.wait_ge(S.xfp, n_all)
+        for b in range(4):
+            product_s(1, b)
+        te.wait_ge(S.zqx, 1)
+        te.wait_ge(S.xtc, n_hi)
+        te.wait_ge(S.xtp, n_hi)
+        for b in range(4):
+            te.wait_ge(S["cp%d" % b], 1)
+            product_s(0, b)
 
-    for b in (0, 1):
-        v.wait_ge(S["mp%d" % b], 1)
-        v.tensor_copy(cut(T.pp, b), bank(b)).then_inc(S["cp%d" % b], 1)
-    a.wait_ge(S.ofs, 1)
-    for h in (0, 1):
-        if h:
-            for b in (2, 3):
-                a.wait_ge(S["mp%d" % b], 1)
-                a.activation(cut(T.pp, b), bank(b), copy).then_inc(S["cp%d" % b], 1)
-        for b in (2 * h, 2 * h + 1):
+        v.wait_ge(S.ckp, 1)
+        v.wait_ge(S.aqf, n_all)
+        lists(1)
+        copy_p(v, 0)
+        copy_p(v, 1)
+        v.wait_ge(S.cqp, 1)
+        v.wait_ge(S.aqt, n_hi)
+        lists(0)
+        copy_p(a, 2)
+        copy_p(a, 3)
+        for q in (1, 0):
+            a.wait_ge(S["ofs%d" % q], 1)
+            for b in range(4):
+                a.wait_ge(S["cp%d" % b], 1)
+                gather(q, b)
+        finish(1, (0, 1))
+        finish(1, (2, 3))
+        pack(1, 0, 256, 4, "qa1")
+        finish(0, (0, 1))
+        finish(0, (2, 3))
+        pack(0, 128, 128, 4, "qb0")
+        pack(0, 0, 128, 4, "qa0")
+        send_a("qa1", 1, (0, L0, r3[0]), (1, L1, r3[1]))
+        send_a("qb0", 0, (1, ALL, oth))
+    else:
+        if core == G:
+            q, kn = 1, n_hi
+            q_from = [("aqf", 2 * n_lo)]
+            rt_from = [("xa" + w, n_all) for w in "cp"]
+            qx_from = [("xf" + w, 2 * n_lo) for w in "cp"]
+        else:
+            q, kn = 0, n_lo
+            q_from = [("aqo", n_hi), ("aqt", n_lo)]
+            rt_from = [("xa" + w, n_lo) for w in "cp"]
+            qx_from = [(x + w, n_hi) for x in ("xo", "xt") for w in "cp"]
+        v.wait_ge(S.akp, kn)
+        v.tensor_copy(T.kpf[:], T.kpi[:]).then_inc(S.ckp, 1)
+        for sem, val in q_from + [("ckp", 1)]:
+            v.wait_ge(S[sem], val)
+        lists(q)
+        for sem, val in rt_from + [("kpk", kn), ("kh1", kn)]:
+            te.wait_ge(S[sem], val)
+        product_p(0)
+        product_p(1)
+        te.wait_ge(S.kh2, kn)
+        product_p(2)
+        product_p(3)
+        for sem, val in qx_from:
+            te.wait_ge(S[sem], val)
+        for b in range(4):
+            product_s(q, b)
+        for b in (0, 1, 2):
+            copy_p(v, b)
+        a.wait_ge(S["ofs%d" % q], 1)
+        for b in (0, 1):
             a.wait_ge(S["cp%d" % b], 1)
-            a.activation(cut(T.pg, b), cut(T.pp, b).indirect(T.off[:, 16 * b:16 * b + 16]), copy).then_inc(S["ga%d" % b], 1)
-    for b in range(4):
-        v.wait_ge(S["ms%d" % b], 1)
-        v.wait_ge(S["ga%d" % b], 1)
-        v.tensor_tensor(T.hh[:, b:1024:4], bank(4 + b), cut(T.pg, b), add).then_inc(S["ad%d" % b], 1)
-        v.wait_ge(S["ad%d" % b], 1)
-        v.tensor_scalar(T.hh[:, b:1024:4], T.hh[:, b:1024:4], 0.0, 0.03125, mx, mult).then_inc(S.clp, 1)
-    v.wait_ge(S.clp, 4)
-    v.quantize_mx(T.kc[:, 0:256], T.ks[:, 0:256], T.hh[:, 0:1024]).then_inc(S.qa, 1)
-
-    A0 = 256 * srank
-    s = S["av%d" % srank]
-    if is_rank:
-        g.wait_ge(S.qa, 1)
-        send(tr(HI, s, code(T.kc, 128, 384), [(oth, code(T.lc, A0, A0 + 256))]))
-        send(tr(HI, s, T.ks[:, 128:384], [(oth, T.ls[:, A0:A0 + 256])]))
-    else:
-        def both(own_ap, oth_ap, land):
-            send(tr(LO, s, own_ap, [(own, land)]), tr(HI, s, oth_ap, [(oth, land)]))
-        g.wait_ge(S.kvc, n_lo)
-        both(code(T.kc, 256, 384), code(T.kc, 256, 384), code(T.lc, A0 + 128, A0 + 256))
-        g.wait_ge(S.kvp, n_lo)
-        both(T.ks[:, 256:384], T.ks[:, 256:384], T.ls[:, A0 + 128:A0 + 256])
-        g.wait_ge(S.qa, 1)
-        both(code(T.kc, 0, 128), code(T.kc, 128, 256), code(T.lc, A0, A0 + 128))
-        both(T.ks[:, 0:128], T.ks[:, 128:256], T.ls[:, A0:A0 + 128])
+            gather(q, b)
+        copy_p(a, 3)
+        a.wait_ge(S.cp2, 1)
+        a.wait_ge(S.cp3, 1)
+        for i in (0, 128):
+            for b in (2, 3):
+                gather(q, b, i, 128, i > 0)
+        finish(q, (0, 1))
+        finish(q, (2, 3), 0, 128)
+        pack(q, 0, 128, 4, "qa%d" % q)
+        finish(q, (2, 3), 128, 128, True)
+        pack(q, 128, 128, 6, "qb%d" % q)
+        m, to = (LO, r2) if core == G else (ALL, (own, oth))
+        send_a("qa%d" % q, q, (0, m, to[0]))
+        send_a("qb%d" % q, q, (1, m, to[1]))
 
     if is_rank:
-        y = T.ps[:, 0:128]
-        te.wait_ge(S.qa, 1)
-        te.wait_ge(S.zvv, 1)
-        te.matmul_mx(y, T.kc[:, 256:384], T.ks[:, 256:384], T.kc[:, 0:128], T.ks[:, 0:128], True, False)
-        order = [oth] + [rank_at(me - k, e) for k in (1, 2, 3) for e in (d, 1 - d)]
-        for i, r in enumerate(order):
-            k = T.rank_of(r)
-            te.wait_ge(S["av%d" % k], 2 * n_hi if r == oth else 4 * n_lo if topo.die(r) == d else 4 * n_hi)
-            c, last = 256 * k, i == len(order) - 1
-            m = te.matmul_mx(y, T.lc[:, c + 128:c + 256], T.ls[:, c + 128:c + 256], T.lc[:, c:c + 128], T.ls[:, c:c + 128],
-                             False, last)
+        y = bank(4, 0, 128)
+        te.wait_ge(S.ad10, 1)
+        order = [(r1[0], n_lo, n_l2), (r1[1], n_lo, n_l2), (own, 0, 0), (oth, n_hi, n_all),
+                 (r3[0], n_all, n_all), (r3[1], n_all, n_all), (r2[0], n_lo, n_lo), (r2[1], n_lo, n_lo)]
+        for i, (r, nv, na) in enumerate(order):
+            if r == own:
+                te.wait_ge(S.qa0, 1)
+                te.wait_ge(S.zvv, 1)
+                ops = T.kc[:, V0:V1], T.ks[:, V0:V1], T.kc[:, 0:128], T.ks[:, 0:128]
+            else:
+                k = T.rank_of(r)
+                te.wait_ge(S["vs%d" % k], 2 * nv)
+                te.wait_ge(S["av%d" % k], 2 * na)
+                (i0, i1), (j0, j1) = land(k, 1), land(k, 0)
+                ops = T.lc[:, i0:i1], T.ls[:, i0:i1], T.lc[:, j0:j1], T.ls[:, j0:j1]
+            m = te.matmul_mx(y, *ops, i == 0, i == len(order) - 1)
         m.then_inc(S.yd, 1)
         v.wait_ge(S.yd, 1)
         v.tensor_copy(T.yo[:], y).then_inc(S.yc, 1)

from concourse.bass import DstId, RemoteDMATransfer
from concourse.mybir import dt, AluOpType, ActivationFunctionType

C4, U8 = "float8_e4m3fn_x4", "uint8"
SCRATCH = {
    "xb": ("sbuf", [128, 1536], "bfloat16"),
    "kb": ("sbuf", [128, 2560], "bfloat16"),
    "xc": ("sbuf", [128, 768], C4),
    "xs": ("sbuf", [128, 768], U8),
    "kc": ("sbuf", [128, 1152], C4),
    "ks": ("sbuf", [128, 1152], U8),
    "lc": ("sbuf", [128, 2048], C4),
    "ls": ("sbuf", [128, 2048], U8),
    "qpi": ("sbuf", [128, 8], "int32"),
    "qp16": ("sbuf", [128, 32], "uint16"),
    "kpi": ("sbuf", [128, 4], "int32"),
    "kpf": ("sbuf", [128, 4], "float32"),
    "dd": ("sbuf", [128, 128], "float32"),
    "off": ("sbuf", [128, 128], "uint16"),
    "pp": ("sbuf", [128, 1024], "float32"),
    "pg": ("sbuf", [128, 2048], "float32"),
    "hh": ("sbuf", [128, 2048], "bfloat16"),
    "yo": ("sbuf", [128, 128], "float32"),
    "ps": ("psum", [128, 4096], "float32"),
}
PIECES = {"h1": (640, 896), "pk": (640, 1152), "h2": (896, 1152)}
SEMAPHORES = (["lkp", "lqp", "lqx", "lrt", "lvv", "lk0", "lk1", "ckp", "cqp", "zqx", "zrt", "zvv", "zk0", "zk1",
               "akp", "aqo", "aqt", "aqf", "xoc", "xop", "xac", "xap", "xtc", "xtp", "xfc", "xfp",
               "vfc", "vfp", "vwc", "vwp", "sent", "yd", "yc", "yst"]
              + ["k" + w for w in PIECES]
              + ["%s%d" % (n, b) for n in ("mp", "cp") for b in range(4)]
              + ["%s%d%d" % (n, q, b) for n in ("ms", "ga", "ad") for q in (0, 1) for b in range(4)]
              + ["%s%d" % (n, b) for n in ("gb", "ae") for b in (2, 3)]
              + ["%s%d" % (n, q) for n in ("dl", "ofs", "clp", "qa", "qb") for q in (0, 1)]
              + ["%s%d" % (n, s) for n in ("av", "vs") for s in range(8)])


def rank_program(g, core, T, topo):
    S = T.sem
    chips = []
    for c in T.cores:
        if topo.chip(c) not in chips:
            chips.append(topo.chip(c))
    if topo.chip(core) not in chips:
        return
    n = len(chips)

    def rank_at(i, d):
        return [c for c in T.cores if topo.chip(c) == chips[i % n] and topo.die(c) == d][0]

    def helpers(r):
        return [c for c in topo.cores_of(r) if topo.die(c) == topo.die(r) and c != r]

    me, d = chips.index(topo.chip(core)), topo.die(core)
    own, oth = rank_at(me, d), rank_at(me, 1 - d)
    F, G, W = helpers(own)
    oW = helpers(oth)[2]
    lo = topo.engines(core, rank_at(me + 1, d))
    near = topo.engines(core, own if core != own else oth)
    hi = [e for e in near if e not in lo]
    LO, HI, ALL, L0, L1 = [sum(1 << e for e in es) for es in (lo, hi, near, lo[:len(lo) // 2], lo[len(lo) // 2:])]
    n_lo, n_hi, n_all, n_l2 = len(lo), len(hi), len(near), len(lo) // 2
    is_rank = core == own
    src = rank_at(me - 1, d) if core == W else own
    srank = T.rank_of(src)
    r1, r2, r3 = [[rank_at(me + k, e) for e in (d, 1 - d)] for k in (1, 2, 3)]
    f1, w1 = helpers(r1[0])[0], helpers(r1[0])[2]
    far = [helpers(r)[1] for r in r2]
    sent = [0]

    def tr(mask, sem, src_ap, dests):
        ids = []
        for c, _ in dests:
            rid, pid, _e = topo.addr(c)
            ids.append(DstId(rid=rid, pnc=pid))
        sent[0] += bin(mask).count("1")
        return RemoteDMATransfer(dst_ids=ids, dma_engine_mask=mask, remote_sem=sem, srcs=[src_ap], dsts=[ap for _, ap in dests])

    def send(*ts):
        g.remote_dma_fused(list(ts), local_sem=S.sent)

    def cols(x, i, j, w):
        return T[x + "c"][:, i:j].bitcast(dt.uint8) if w == "c" else T[x + "s"][:, i:j]

    def land(s, part):
        c = 256 * s + 128 * part
        return c, c + 128

    sub, add, mx, mn, mult = AluOpType.subtract, AluOpType.add, AluOpType.max, AluOpType.min, AluOpType.mult
    copy = ActivationFunctionType.Copy
    v, a, te = g.vector, g.scalar, g.tensor
    q4 = [T.qp16[:, 8 * i:8 * i + 8] for i in range(4)]
    X = [(256 + 128 * i, 384 + 128 * i) for i in range(4)]
    V0, V1 = 512, 640
    vs, av = S["vs%d" % srank], S["av%d" % srank]

    def give_v(mask, w, to):
        p, at = cols("k", V0, V1, w), cols("l", *land(srank, 1), w)
        send(tr(mask, vs, p, [(c, at) for c in to]))

    if is_rank:
        a.dma_start(T.kpi[:], T.kp[:]).then_inc(S.lkp, 16)
        for k in range(8):
            (a if k % 2 else g.sync).dma_start(T.qpi[16 * k:16 * k + 16, :], T.qp[:]).then_inc(S.lqp, 16)
        g.sync.dma_start(T.xb[:, 1024:1536], T.qx[:]).then_inc(S.lqx, 16)
        a.dma_start(T.xb[:, 0:1024], T.rt[:]).then_inc(S.lrt, 16)
        g.sync.dma_start(T.kb[:, 512:1536], T.ky[:, 0:1024]).then_inc(S.lk0, 16)
        a.dma_start(T.kb[:, 1536:2560], T.ky[:, 1024:2048]).then_inc(S.lk1, 16)
        g.sync.dma_start(T.kb[:, 0:512], T.vv[:]).then_inc(S.lvv, 16)

        v.wait_ge(S.lqp, 128)
        v.tensor_copy(q4[0], T.qpi[:]).then_inc(S.cqp, 1)
        v.wait_ge(S.lkp, 16)
        v.tensor_copy(T.kpf[:], T.kpi[:]).then_inc(S.ckp, 1)
        v.wait_ge(S.lqx, 16)
        v.quantize_mx(T.xc[:, 256:384], T.xs[:, 256:384], T.xb[:, 1024:1536]).then_inc(S.zqx, 1)
        v.wait_ge(S.lrt, 16)
        v.quantize_mx(T.xc[:, 0:256], T.xs[:, 0:256], T.xb[:, 0:1024]).then_inc(S.zrt, 1)
        v.wait_ge(S.lk0, 16)
        v.quantize_mx(T.kc[:, 640:896], T.ks[:, 640:896], T.kb[:, 512:1536]).then_inc(S.zk0, 1)
        v.wait_ge(S.lk1, 16)
        v.quantize_mx(T.kc[:, 896:1152], T.ks[:, 896:1152], T.kb[:, 1536:2560]).then_inc(S.zk1, 1)
        v.wait_ge(S.lvv, 16)
        v.quantize_mx(T.kc[:, V0:V1], T.ks[:, V0:V1], T.kb[:, 0:512]).then_inc(S.zvv, 1)

        g.wait_ge(S.lkp, 16)
        send(tr(LO, S.akp, T.kpi[:], [(w1, T.kpi[:])]), tr(HI, S.akp, T.kpi[:], [(G, T.kpi[:])]))
        g.wait_ge(S.cqp, 1)
        send(tr(LO, S.aqo, q4[0], [(f1, q4[0])]), tr(HI, S.aqo, q4[0], [(G, q4[0]), (W, q4[0])]))
        g.wait_ge(S.zqx, 1)
        for w in "cp":
            p = cols("x", *X[0], w)
            send(tr(LO, S["xo" + w], p, [(f1, p)]), tr(HI, S["xo" + w], p, [(W, p)]))
        g.wait_ge(S.zrt, 1)
        for w in "cp":
            p = cols("x", 0, 256, w)
            send(tr(ALL, S["xa" + w], p, [(G, p)]))
        for w in PIECES:
            if w != "h2":
                g.wait_ge(S.zk0 if w == "h1" else S.zk1, 1)
            p = cols("k", *PIECES[w], "p" if w == "pk" else "c")
            send(tr(LO, S["k" + w], p, [(w1, p)]), tr(HI, S["k" + w], p, [(G, p)]))
        g.wait_ge(S.zvv, 1)
        for w in "cp":
            p = cols("k", V0, V1, w)
            send(tr(LO, S["vw" + w], p, [(w1, p)]), tr(HI, S["vf" + w], p, [(F, p), (G, p)]))
        for w in "cp":
            give_v(HI, w, [oth])

    elif core == F:
        g.wait_ge(S.aqo, n_lo)
        send(tr(LO, S.aqf, q4[0], [(own, q4[2])]), tr(HI, S.aqf, q4[0], [(oth, q4[3])]))
        for w in "cp":
            g.wait_ge(S["xo" + w], n_lo)
            p = cols("x", *X[0], w)
            send(tr(LO, S["xf" + w], p, [(own, cols("x", *X[2], w))]), tr(HI, S["xf" + w], p, [(oth, cols("x", *X[3], w))]))
        for w in "cp":
            g.wait_ge(S["vf" + w], n_hi)
            give_v(LO, w, r3)
        g.wait_ge(S.sent, sent[0])
        return
    elif core == G:
        g.wait_ge(S.aqo, n_hi)
        send(tr(LO, S.aqf, q4[0], [(far[0], q4[2]), (far[1], q4[3])]))
        for w in "cp":
            g.wait_ge(S["xa" + w], n_all)
            p = cols("x", 0, 256, w)
            send(tr(LO, S["xa" + w], p, [(W, p)]))
        for w in "cp":
            g.wait_ge(S["vf" + w], n_hi)
            give_v(LO, w, r2)
    elif core == W:
        g.wait_ge(S.aqo, n_hi)
        send(tr(LO, S.aqt, q4[0], [(oW, q4[1])]), tr(HI, S.aqt, q4[0], [(oth, q4[1])]))
        for w in "cp":
            g.wait_ge(S["xo" + w], n_hi)
            p, to = cols("x", *X[0], w), cols("x", *X[1], w)
            send(tr(LO, S["xf" + w], p, [(far[i], cols("x", *X[2 + i], w)) for i in (0, 1)]),
                 tr(HI, S["xt" + w], p, [(oW, to), (oth, to)]))
        for w in "cp":
            g.wait_ge(S["vw" + w], n_lo)
            give_v(ALL, w, (own, oth))

    def lists(q):
        for b in range(4):
            o = 64 * q + 16 * b
            v.tensor_scalar(T.dd[:, o:o + 16], T.qp16[:, 16 * q:16 * q + 16], T.kpf[:, b:b + 1], -128.0, sub, mx).then_inc(S["dl%d" % q], 1)
        v.wait_ge(S["dl%d" % q], 4)
        v.tensor_scalar(T.off[:, 64 * q:64 * q + 64], T.dd[:, 64 * q:64 * q + 64], 127.0, 128.0, mn, add).then_inc(S["ofs%d" % q], 1)

    def stat(b):
        return T.kc[:, 640 + 128 * b:768 + 128 * b], T.ks[:, 640 + 128 * b:768 + 128 * b]

    def bank(b, i=0, w=256):
        return T.ps[:, 512 * b + i:512 * b + i + w]

    def sbank(q, b):
        return b if is_rank and q == 0 else 4 + b

    def product_p(b):
        te.matmul_mx(bank(b), *stat(b), T.xc[:, 0:256], T.xs[:, 0:256], True, True).then_inc(S["mp%d" % b], 1)

    def product_s(q, b):
        i = 256 + 256 * q
        te.matmul_mx(bank(sbank(q, b)), *stat(b), T.xc[:, i:i + 256], T.xs[:, i:i + 256], True, True).then_inc(S["ms%d%d" % (q, b)], 1)

    def copy_p(eng, b):
        p = T.pp[:, 256 * b:256 * b + 256]
        eng.wait_ge(S["mp%d" % b], 1)
        (v.tensor_copy(p, bank(b)) if eng is v else a.activation(p, bank(b), copy)).then_inc(S["cp%d" % b], 1)

    def gather(q, b, i=0, w=256, second=False):
        o, r = 64 * q + 16 * b + i // 16, 1024 * q + 256 * b + i
        done = S["gb%d" % b] if second else S["ga%d%d" % (q, b)]
        a.activation(T.pg[:, r:r + w], T.pp[:, 256 * b:256 * b + 256].indirect(T.off[:, o:o + w // 16]), copy).then_inc(done, 1)

    def finish(q, bs, i=0, w=256, second=False):
        o = 1024 * q + 4 * i
        added = {b: S["ae%d" % b] if second else S["ad%d%d" % (q, b)] for b in bs}
        for b in bs:
            r = 1024 * q + 256 * b + i
            v.wait_ge(S["ms%d%d" % (q, b)], 1)
            v.wait_ge(S["gb%d" % b] if second else S["ga%d%d" % (q, b)], 1)
            v.tensor_tensor(T.hh[:, o + b:o + 4 * w:4], bank(sbank(q, b), i, w), T.pg[:, r:r + w], add).then_inc(added[b], 1)
        for b in bs:
            h = T.hh[:, o + b:o + 4 * w:4]
            v.wait_ge(added[b], 1)
            v.tensor_scalar(h, h, 0.0, 0.03125, mx, mult).then_inc(S["clp%d" % q], 1)

    def pack(q, i, w, clipped, name):
        v.wait_ge(S["clp%d" % q], clipped)
        k, t = 256 * q + i, 1024 * q + 4 * i
        v.quantize_mx(T.kc[:, k:k + w], T.ks[:, k:k + w], T.hh[:, t:t + 4 * w]).then_inc(S[name], 1)

    def send_a(name, q, *ts):
        g.wait_ge(S[name], 1)
        for w in "cp":
            to = cols("l", *land(srank, 0), w)
            send(*[tr(m, av, cols("k", 256 * q + 128 * i, 256 * q + 128 * i + 128, w), [(c, to)]) for i, m, c in ts])

    if is_rank:
        te.wait_ge(S.zrt, 1)
        te.wait_ge(S.zk0, 1)
        product_p(0)
        product_p(1)
        te.wait_ge(S.zk1, 1)
        product_p(2)
        product_p(3)
        te.wait_ge(S.xfc, n_all)
        te.wait_ge(S.xfp, n_all)
        for b in range(4):
            product_s(1, b)
        te.wait_ge(S.zqx, 1)
        te.wait_ge(S.xtc, n_hi)
        te.wait_ge(S.xtp, n_hi)
        for b in range(4):
            te.wait_ge(S["cp%d" % b], 1)
            product_s(0, b)

        v.wait_ge(S.ckp, 1)
        v.wait_ge(S.aqf, n_all)
        lists(1)
        copy_p(v, 0)
        copy_p(v, 1)
        v.wait_ge(S.cqp, 1)
        v.wait_ge(S.aqt, n_hi)
        lists(0)
        copy_p(a, 2)
        copy_p(a, 3)
        for q in (1, 0):
            a.wait_ge(S["ofs%d" % q], 1)
            for b in range(4):
                a.wait_ge(S["cp%d" % b], 1)
                gather(q, b)
        finish(1, (0, 1))
        finish(1, (2, 3))
        pack(1, 0, 256, 4, "qa1")
        finish(0, (0, 1))
        finish(0, (2, 3))
        pack(0, 128, 128, 4, "qb0")
        pack(0, 0, 128, 4, "qa0")
        send_a("qa1", 1, (0, L0, r3[0]), (1, L1, r3[1]))
        send_a("qb0", 0, (1, ALL, oth))
    else:
        if core == G:
            q, kn = 1, n_hi
            q_from = [("aqf", 2 * n_lo)]
            rt_from = [("xa" + w, n_all) for w in "cp"]
            qx_from = [("xf" + w, 2 * n_lo) for w in "cp"]
        else:
            q, kn = 0, n_lo
            q_from = [("aqo", n_hi), ("aqt", n_lo)]
            rt_from = [("xa" + w, n_lo) for w in "cp"]
            qx_from = [(x + w, n_hi) for x in ("xo", "xt") for w in "cp"]
        v.wait_ge(S.akp, kn)
        v.tensor_copy(T.kpf[:], T.kpi[:]).then_inc(S.ckp, 1)
        for sem, val in q_from + [("ckp", 1)]:
            v.wait_ge(S[sem], val)
        lists(q)
        for sem, val in rt_from + [("kpk", kn), ("kh1", kn)]:
            te.wait_ge(S[sem], val)
        product_p(0)
        product_p(1)
        te.wait_ge(S.kh2, kn)
        product_p(2)
        product_p(3)
        for sem, val in qx_from:
            te.wait_ge(S[sem], val)
        for b in range(4):
            product_s(q, b)
        for b in (0, 1, 2):
            copy_p(v, b)
        a.wait_ge(S["ofs%d" % q], 1)
        for b in (0, 1):
            a.wait_ge(S["cp%d" % b], 1)
            gather(q, b)
        copy_p(a, 3)
        a.wait_ge(S.cp2, 1)
        a.wait_ge(S.cp3, 1)
        for i in (0, 128):
            for b in (2, 3):
                gather(q, b, i, 128, i > 0)
        finish(q, (0, 1))
        finish(q, (2, 3), 0, 128)
        pack(q, 0, 128, 4, "qa%d" % q)
        finish(q, (2, 3), 128, 128, True)
        pack(q, 128, 128, 6, "qb%d" % q)
        m, to = (LO, r2) if core == G else (ALL, (own, oth))
        send_a("qa%d" % q, q, (0, m, to[0]))
        send_a("qb%d" % q, q, (1, m, to[1]))

    if is_rank:
        y = bank(4, 0, 128)
        te.wait_ge(S.ad10, 1)
        order = [(r1[0], n_lo, n_l2), (r1[1], n_lo, n_l2), (own, 0, 0), (oth, n_hi, n_all),
                 (r3[0], n_all, n_all), (r3[1], n_all, n_all), (r2[0], n_lo, n_lo), (r2[1], n_lo, n_lo)]
        for i, (r, nv, na) in enumerate(order):
            if r == own:
                te.wait_ge(S.qa0, 1)
                te.wait_ge(S.zvv, 1)
                ops = T.kc[:, V0:V1], T.ks[:, V0:V1], T.kc[:, 0:128], T.ks[:, 0:128]
            else:
                k = T.rank_of(r)
                te.wait_ge(S["vs%d" % k], 2 * nv)
                te.wait_ge(S["av%d" % k], 2 * na)
                (i0, i1), (j0, j1) = land(k, 1), land(k, 0)
                ops = T.lc[:, i0:i1], T.ls[:, i0:i1], T.lc[:, j0:j1], T.ls[:, j0:j1]
            m = te.matmul_mx(y, *ops, i == 0, i == len(order) - 1)
        m.then_inc(S.yd, 1)
        v.wait_ge(S.yd, 1)
        v.tensor_copy(T.yo[:], y).then_inc(S.yc, 1)
        g.sync.wait_ge(S.yc, 1)
        g.sync.dma_start(T.y[:], T.yo[:]).then_inc(S.yst, 16)
        g.sync.wait_ge(S.yst, 16)
    g.wait_ge(S.sent, sent[0])
